import numpy as np
import ml_dtypes


def mxq(x, axis, fmt="e4m3"):
    dtype, down = {"e4m3": (ml_dtypes.float8_e4m3fn, 7), "e5m2": (ml_dtypes.float8_e5m2, 14)}[fmt]
    v = np.moveaxis(np.asarray(x, np.float32).astype(ml_dtypes.bfloat16).astype(np.float64), axis, -1)
    blocks = v.reshape(v.shape[:-1] + (-1, 32))
    amax = np.abs(blocks).max(-1, keepdims=True)
    byte = np.maximum(np.where(amax > 0, np.frexp(amax)[1] - 1 + 127, 0) - down, 1)
    scale = np.exp2(byte - 127.0)
    codes = (blocks / scale).astype(np.float32).astype(dtype).astype(np.float64)
    return np.moveaxis((codes * scale).reshape(v.shape), -1, axis)


WIDE = False


def mx_kscale(k):
    if not WIDE:
        return np.ones(k)
    levels = np.array([10, -10, 5, -5, 0])
    if k % 512:
        return np.exp2(np.random.permutation(np.resize(levels, k // 32))).repeat(32)
    a = np.empty((k // 512, 16))
    for p in range(k // 512):
        a[p, :8] = np.random.permutation(np.resize(levels, 8))
        for g in range(8):
            far = levels[np.abs(levels - a[p, g]) >= 10]
            a[p, g + 8] = far[np.random.randint(len(far))]
    return np.exp2(a.ravel()).repeat(32)


def f64(x):
    return np.asarray(x).astype(np.float64)


def striped(idx):
    return np.tile(idx.reshape(-1, 16).T, (8, 1)).astype(np.uint16)


def unstriped(offs):
    return offs[:16].T.reshape(-1).astype(np.int64)


E2M1 = np.array([0.0, 0.5, 1.0, 1.5, 2.0, 3.0, 4.0, 6.0, -0.0, -0.5, -1.0, -1.5, -2.0, -3.0, -4.0, -6.0])


def pack_weight(w, fmt):
    k, n = w.shape
    w = f64(np.asarray(w, np.float32).astype(ml_dtypes.bfloat16)).reshape(k // 32, 32, n)
    amax = np.abs(w).max(1)
    if fmt == "e4m3":
        byte = np.frexp(amax)[1] - 1 + 127 - 7
    else:
        mant, ex = np.frexp(amax / 6.0)
        byte = np.where(mant > 0.5, ex, ex - 1) + 127
    byte = np.clip(np.where(amax > 0, byte, 1), 1, 254)
    scaled = (w * np.exp2(127.0 - byte)[:, None, :]).reshape(k, n).astype(np.float32)
    by_word = np.ascontiguousarray(scaled.reshape(k // 512, 128, 4, n).transpose(0, 1, 3, 2))
    if fmt == "e4m3":
        words = by_word.astype(ml_dtypes.float8_e4m3fn).view(np.uint8)
    else:
        c = by_word.astype(ml_dtypes.float4_e2m1fn).view(np.uint8) & 0xF
        words = (c[..., 0::2] | (c[..., 1::2] << 4)).reshape(k // 512, 128, 2 * n)
    return np.ascontiguousarray(words), np.ascontiguousarray(byte.astype(np.uint8).reshape(k // 512, 16, n))


def unpack_weight(words, scales, fmt):
    g, _, n = scales.shape
    words = np.ascontiguousarray(words).reshape(g, 128, n, -1)
    if fmt == "e4m3":
        vals = words.view(ml_dtypes.float8_e4m3fn).astype(np.float64)
    else:
        nib = np.empty((g, 128, n, 4), np.uint8)
        nib[..., 0::2] = words & 0xF
        nib[..., 1::2] = words >> 4
        vals = E2M1[nib]
    vals = vals * np.repeat(np.exp2(scales.astype(np.float64) - 127.0), 8, axis=1)[..., None]
    return vals.transpose(0, 1, 3, 2).reshape(g * 512, n)


def relu(v):
    return np.maximum(v, 0.0)


K, T, Q, E, C, D, H = 512, 768, 512, 4, 128, 256, 512
N = 256


def by_expert(wq, xq, C):
    return np.concatenate([wq[e].T @ xq[:, e * C:(e + 1) * C] for e in range(E)], axis=1)


def setup_inputs():
    n = np.random.standard_normal
    s = mx_kscale(K)
    u = mx_kscale(H)
    slot_token = np.random.permutation(T)[:E * C]
    slots2 = np.concatenate([np.random.permutation(Q)[:D] for e in range(E)])
    x = pack_weight(n((K, Q)) * s[:, None], "e4m3")
    w1 = [pack_weight(m, "e4m3") for m in n((E, K, H)) / np.sqrt(K) / s[None, :, None]]
    w3 = [pack_weight(m, "e4m3") for m in n((E, K, H)) / np.sqrt(K) / s[None, :, None] * u]
    w2 = [pack_weight(m, "e4m3") for m in n((E, H, N)) / np.sqrt(H) / u[None, :, None]]
    return {
        "x_words": x[0],
        "x_scales": x[1],
        "xo": (n((K, T)) * s[:, None]).astype(np.float32),
        "w1_words": np.stack([m[0] for m in w1]),
        "w1_scales": np.stack([m[1] for m in w1]),
        "w3_words": np.stack([m[0] for m in w3]),
        "w3_scales": np.stack([m[1] for m in w3]),
        "w2_words": np.stack([m[0] for m in w2]),
        "w2_scales": np.stack([m[1] for m in w2]),
        "gate": np.tile(np.random.uniform(0.2, 1.0, E * C), (128, 1)).astype(np.float32),
        "offs": striped(slot_token),
        "offs2": striped(slots2),
    }


def reference(x_words, x_scales, xo, w1_words, w1_scales, w3_words, w3_scales, w2_words, w2_scales, gate, offs, offs2):
    w1 = np.stack([unpack_weight(w1_words[e], w1_scales[e], "e4m3") for e in range(E)])
    w3 = np.stack([unpack_weight(w3_words[e], w3_scales[e], "e4m3") for e in range(E)])
    w2 = np.stack([unpack_weight(w2_words[e], w2_scales[e], "e4m3") for e in range(E)])
    idx, idx2 = unstriped(offs), unstriped(offs2)
    xq = mxq(f64(xo)[:, idx], 0, "e4m3")
    rq = unpack_weight(x_words, x_scales, "e4m3")[:, idx2]
    h = relu(by_expert(w1, xq, C)) * by_expert(w3, xq, C)
    y = by_expert(w2, mxq(h, 0, "e4m3"), C)
    h = relu(by_expert(w1, rq, D)) * by_expert(w3, rq, D)
    z = by_expert(w2, mxq(h, 0, "e4m3"), D)
    own = np.zeros((N, T))
    own[:, idx] = f64(gate[:1]) * y
    return np.concatenate([own, z], axis=1)

@@ -1,0 +1,252 @@
+from contextlib import ExitStack
+
+import concourse.mybir as mybir
+from concourse.masks import make_identity
+
+K, T, Q, E, C, D, H, N = 512, 768, 512, 4, 128, 256, 512, 256
+FLOPS = 2 * E * (C + D) * (2 * K * H + H * N)
+
+F32 = mybir.dt.float32
+BF16 = mybir.dt.bfloat16
+I32 = mybir.dt.int32
+U32 = mybir.dt.uint32
+U16 = mybir.dt.uint16
+U8 = mybir.dt.uint8
+FP8X4 = mybir.dt.float8_e4m3fn_x4
+MULT = mybir.AluOpType.mult
+RELU = mybir.ActivationFunctionType.Relu
+
+P = 128
+PAIR = 2 * P
+
+
+def tile_moe_loc_glu_relu_kernel(
+    tc, x_words, x_scales, xo, w1_words, w1_scales, w3_words, w3_scales, w2_words, w2_scales, gate, offs, offs2, out
+):
+    nc = tc.nc
+    with ExitStack() as ctx:
+        keep = ctx.enter_context(tc.tile_pool(name="keep", bufs=1))
+        ring = ctx.enter_context(tc.tile_pool(name="ring", bufs=3))
+        psum = ctx.enter_context(tc.psum_pool(name="psum", bufs=1))
+
+        def held(shape, dtype, name):
+            return keep.tile(shape, dtype, name=name, align_bytes=64)
+
+        def as_words(dram):
+            return dram.rearrange("p n t -> p (n t)").bitcast(I32)
+
+        own_list = keep.tile([P, E * C // 16], U16, name="own_list")
+        far_list = keep.tile([P, E * D // 16], U16, name="far_list")
+        far_words = held([P, Q], I32, "far_words")
+        far_scales = held([P, Q], U8, "far_scales")
+        xo_raw = [held([P, 2, T], F32, "xo_raw%d" % u) for u in range(2)]
+        w1 = [held([P, H], I32, "w1_%d" % e) for e in range(E)]
+        w3 = [held([P, H], I32, "w3_%d" % e) for e in range(E)]
+        w2 = held([P, E, N], I32, "w2")
+        w1s = held([P, H], U8, "w1s")
+        w3s = held([P, H], U8, "w3s")
+        w2s = held([P, N], U8, "w2s")
+        gate_sb = held([P, E * C], F32, "gate_sb")
+        ident = held([P, P], F32, "ident")
+        own_out = [held([P, T], F32, "own_out%d" % h) for h in range(2)]
+
+        for plane in (far_scales, w1s, w3s, w2s):
+            nc.vector.memset(plane[:].bitcast(I32), 0)
+
+        def load_scales(queue, plane, dram):
+            for q in range(4):
+                queue.dma_start(plane[32 * q : 32 * q + 16, :].bitcast(I32), dram[:, 0, 4 * q : 4 * q + 4, :].bitcast(I32))
+
+        def load_first_layer(e):
+            nc.sync.dma_start(w1[e][:], as_words(w1_words[e, 0]))
+            nc.sync.dma_start(w3[e][:], as_words(w3_words[e, 0]))
+
+        nc.sync.dma_start(far_list[:], offs2)
+        nc.sync.dma_start(far_words[:], as_words(x_words[0]))
+        for q in range(4):
+            nc.sync.dma_start(far_scales[32 * q : 32 * q + 4, :].bitcast(I32), x_scales[0, 4 * q : 4 * q + 4, :].bitcast(I32))
+        xo_rows = xo.rearrange("(p j) c -> p j c", j=4)
+        for u in range(2):
+            nc.sync.dma_start(xo_raw[u][:], xo_rows[:, 2 * u : 2 * u + 2, :])
+        load_scales(nc.sync, w1s, w1_scales)
+        load_first_layer(0)
+        nc.sync.dma_start(own_list[:], offs)
+        load_first_layer(1)
+        load_scales(nc.sync, w2s, w2_scales)
+        nc.sync.dma_start(w2[:], w2_words[:, 0].rearrange("e p n t -> p e (n t)").bitcast(I32))
+        load_first_layer(2)
+        nc.sync.dma_start(gate_sb[:], gate)
+        load_first_layer(3)
+        load_scales(nc.gpsimd, w3s, w3_scales)
+
+        make_identity(nc, ident[:])
+        nc.vector.memset(own_out[0][:], 0.0)
+        nc.scalar.activation(own_out[1][:], own_out[0][:], RELU)
+
+        slot_words = {}
+        slot_scales = {}
+
+        def gather_far(e):
+            words = held([P, D], U32, "fw%d" % e)
+            scales = held([P, D], U8, "fs%d" % e)
+            cols = far_list[:, e * D // 16 : (e + 1) * D // 16]
+            nc.vector.tensor_copy(words[:], far_words[:].bitcast(U32).indirect(cols))
+            nc.vector.tensor_copy(scales[:], far_scales[:].indirect(cols))
+            slot_words["far", e] = words
+            slot_scales["far", e] = scales
+
+        pairs = [held([P, T, 2], BF16, "pairs%d" % u) for u in range(2)]
+
+        def round_own(u):
+            nc.scalar.copy(pairs[u][:], xo_raw[u][:].rearrange("p e c -> p c e"))
+
+        picked = held([P, 2, E * C, 2], BF16, "picked")
+
+        def gather_own(u):
+            window = pairs[u][:].rearrange("p c e -> p (c e)").bitcast(U32)
+            nc.vector.tensor_copy(picked[:, u].rearrange("p c e -> p (c e)").bitcast(U32), window.indirect(own_list[:]))
+
+        grouped = [held([P, PAIR, 2, 2], BF16, "grouped%d" % g) for g in range(2)]
+
+        def interleave_own(g):
+            nc.scalar.copy(grouped[g][:], picked[:, :, g * PAIR : (g + 1) * PAIR, :].rearrange("p u c e -> p c u e"))
+
+        def quantize_own(g):
+            words = held([P, PAIR], U32, "ow%d" % g)
+            scales = held([P, PAIR], U8, "os%d" % g)
+            nc.vector.quantize_mx(words[:].bitcast(FP8X4), scales[:], grouped[g][:].rearrange("p c u e -> p (c u e)"))
+            slot_words["own", g] = words
+            slot_scales["own", g] = scales
+
+        def expert_of(group, half):
+            kind, g = group
+            return g if kind == "far" else 2 * g + half
+
+        hidden = {}
+        sums = {}
+        rectified = {}
+
+        def first_layer(group, half):
+            e = expert_of(group, half)
+            cols = slice(half * P, (half + 1) * P)
+            a1 = psum.tile([P, H], F32, name="a1", bufs=3)
+            a3 = psum.tile([P, H], F32, name="a3", bufs=3)
+            for acc, w, ws in ((a1, w1, w1s), (a3, w3, w3s)):
+                nc.tensor.matmul_mx(
+                    acc[:], lhsT=slot_words[group][:, cols].bitcast(FP8X4), lhsT_scale=slot_scales[group][:, cols],
+                    rhs=w[e][:].bitcast(FP8X4), rhs_scale=ws[4 * e : P, :], start=True, stop=True,
+                )
+            sums[group, half] = (a1, a3)
+
+        def rectify(group, half):
+            gatev = ring.tile([P, 2, P, 2], F32, name="gatev")
+            nc.scalar.activation(gatev[:], sums[group, half][0][:].rearrange("s (p u e) -> s u p e", u=2, e=2), RELU)
+            rectified[group, half] = gatev
+
+        def multiply(group, half):
+            a3 = sums[group, half][1]
+            gatev = rectified[group, half]
+            hid = ring.tile([P, 2, P, 2], BF16, name="hid", bufs=4, align_bytes=64)
+            nc.vector.tensor_tensor(hid[:], a3[:].rearrange("s (p u e) -> s u p e", u=2, e=2), gatev[:], MULT)
+            hidden[group, half] = hid
+
+        turned = {}
+        banks = {}
+
+        def turn(group):
+            bank = psum.tile([P, 2, 2, P], F32, name="turn_bank")
+            for half in range(2):
+                for u in range(2):
+                    nc.tensor.transpose(bank[:, half, u, :], hidden[group, half][:, u].rearrange("s p e -> s (p e)").bitcast(F32), ident[:])
+            banks["turn", group] = bank
+
+        def leave_turn(group):
+            bank = banks["turn", group]
+            hT = ring.tile([P, 2, P, 2], F32, name="hT", align_bytes=64)
+            nc.scalar.copy(hT[:], bank[:].rearrange("p a u s -> p a s u"))
+            turned[group] = hT
+
+        coded = {}
+
+        def quantize_hidden(group):
+            words = ring.tile([P, PAIR], U32, name="hw", align_bytes=64)
+            scales = ring.tile([P, PAIR], U8, name="hs", align_bytes=64)
+            nc.vector.quantize_mx(words[:].bitcast(FP8X4), scales[:], turned[group][:].rearrange("p a s u -> p (a s u)").bitcast(BF16))
+            coded[group] = (words, scales)
+
+        results = {}
+
+        def second_layer(group):
+            words, scales = coded[group]
+            bank = psum.tile([P, 2, PAIR], F32, name="y_bank")
+            spans = [slice(0, PAIR)] if group[0] == "far" else [slice(0, P), slice(P, PAIR)]
+            for h in range(2):
+                rows = slice(h * P, (h + 1) * P)
+                for half, span in enumerate(spans):
+                    e = expert_of(group, half)
+                    nc.tensor.matmul_mx(
+                        bank[:, h, span], lhsT=w2[:, e, rows].bitcast(FP8X4), lhsT_scale=w2s[4 * e : P, rows],
+                        rhs=words[:, span].bitcast(FP8X4), rhs_scale=scales[:, span], start=True, stop=True,
+                    )
+            banks["y", group] = bank
+
+        def leave_second(group):
+            bank = banks["y", group]
+            y = ring.tile([P, 2, PAIR], F32, name="y", bufs=6)
+            nc.scalar.copy(y[:], bank[:])
+            results[group] = y
+            if group[0] == "far":
+                first = T + group[1] * D
+                nc.sync.dma_start(out[:, first : first + D].rearrange("(h p) c -> p h c", h=2), y[:])
+
+        def scatter(e, h):
+            cols = own_list[:, e * C // 16 : (e + 1) * C // 16]
+            y = results["own", e // 2][:, h, (e % 2) * C : (e % 2 + 1) * C]
+            nc.vector.tensor_tensor(own_out[h][:].indirect(cols), y, gate_sb[:, e * C : (e + 1) * C], MULT)
+            if e == E - 1:
+                nc.sync.dma_start(out[h * P : (h + 1) * P, 0:T], own_out[h][:])
+
+        groups = [("far", 0), ("own", 0), ("far", 1), ("own", 1), ("far", 2), ("far", 3)]
+        gather_far(0)
+        round_own(0)
+        round_own(1)
+        gather_far(1)
+        gather_far(2)
+        gather_own(0)
+        gather_own(1)
+
+        fillers = {
+            (0, 1): [(interleave_own, 0), (quantize_own, 0), (interleave_own, 1)],
+            (1, 0): [(quantize_own, 1)],
+            (2, 0): [(gather_far, 3)],
+            (4, 0): [(scatter, 0, 0)],
+            (4, 1): [(scatter, 0, 1)],
+            (4, 2): [(scatter, 1, 0)],
+            (5, 2): [(scatter, 1, 1)],
+            (6, 1): [(scatter, 2, 0)],
+            (7, 0): [(scatter, 3, 0), (scatter, 2, 1), (scatter, 3, 1)],
+        }
+
+        def fill(step, slot):
+            for work, *args in fillers.get((step, slot), []):
+                work(*args)
+
+        def stage(work, step, *args):
+            if 0 <= step < len(groups):
+                work(groups[step], *args)
+
+        for step in range(len(groups) + 2):
+            fill(step, 0)
+            for half in range(2):
+                stage(first_layer, step, half)
+            for half in range(2):
+                stage(rectify, step, half)
+            stage(multiply, step, 0)
+            fill(step, 1)
+            stage(multiply, step, 1)
+            stage(turn, step - 1)
+            stage(second_layer, step - 2)
+            stage(leave_turn, step - 1)
+            stage(leave_second, step - 2)
+            fill(step, 2)
+            stage(quantize_hidden, step - 1)

@@ -40,15 +40,15 @@ def tile_moe_loc_glu_relu_kernel(
         far_words = held([P, Q], I32, "far_words")
         far_scales = held([P, Q], U8, "far_scales")
         xo_raw = [held([P, 2, T], F32, "xo_raw%d" % u) for u in range(2)]
-        w1 = [held([P, H], I32, "w1_%d" % e) for e in range(E)]
-        w3 = [held([P, H], I32, "w3_%d" % e) for e in range(E)]
+        w1 = held([P, E, H], I32, "w1")
+        w3 = held([P, E, H], I32, "w3")
         w2 = held([P, E, N], I32, "w2")
         w1s = held([P, H], U8, "w1s")
         w3s = held([P, H], U8, "w3s")
         w2s = held([P, N], U8, "w2s")
         gate_sb = held([P, E * C], F32, "gate_sb")
         ident = held([P, P], F32, "ident")
-        own_out = [held([P, T], F32, "own_out%d" % h) for h in range(2)]
+        own_out = {0: held([P, T], F32, "own_out0")}
 
         for plane in (far_scales, w1s, w3s, w2s):
             nc.vector.memset(plane[:].bitcast(I32), 0)
@@ -57,59 +57,70 @@ def tile_moe_loc_glu_relu_kernel(
             for q in range(4):
                 queue.dma_start(plane[32 * q : 32 * q + 16, :].bitcast(I32), dram[:, 0, 4 * q : 4 * q + 4, :].bitcast(I32))
 
-        def load_first_layer(e):
-            nc.sync.dma_start(w1[e][:], as_words(w1_words[e, 0]))
-            nc.sync.dma_start(w3[e][:], as_words(w3_words[e, 0]))
+        def load_words(tile, dram, first, last):
+            nc.sync.dma_start(tile[:, first:last, :], dram[first:last, 0].rearrange("e p n t -> p e (n t)").bitcast(I32))
 
+        def load_first_layer(first, last):
+            load_words(w1, w1_words, first, last)
+            load_words(w3, w3_words, first, last)
+
+        xo_rows = xo.rearrange("(p j) c -> p j c", j=4)
+        load_scales(nc.gpsimd, w3s, w3_scales)
+        make_identity(nc, ident[:])
         nc.sync.dma_start(far_list[:], offs2)
         nc.sync.dma_start(far_words[:], as_words(x_words[0]))
         for q in range(4):
             nc.sync.dma_start(far_scales[32 * q : 32 * q + 4, :].bitcast(I32), x_scales[0, 4 * q : 4 * q + 4, :].bitcast(I32))
-        xo_rows = xo.rearrange("(p j) c -> p j c", j=4)
-        for u in range(2):
-            nc.sync.dma_start(xo_raw[u][:], xo_rows[:, 2 * u : 2 * u + 2, :])
-        load_scales(nc.sync, w1s, w1_scales)
-        load_first_layer(0)
+        nc.sync.dma_start(xo_raw[0][:], xo_rows[:, 0 : 2, :])
+        nc.sync.dma_start(xo_raw[1][:], xo_rows[:, 2 : 4, :])
         nc.sync.dma_start(own_list[:], offs)
-        load_first_layer(1)
+        load_scales(nc.sync, w1s, w1_scales)
+        load_first_layer(0, 1)
+        load_first_layer(1, 2)
         load_scales(nc.sync, w2s, w2_scales)
-        nc.sync.dma_start(w2[:], w2_words[:, 0].rearrange("e p n t -> p e (n t)").bitcast(I32))
-        load_first_layer(2)
+        load_words(w2, w2_words, 0, E)
+        load_first_layer(2, 3)
         nc.sync.dma_start(gate_sb[:], gate)
-        load_first_layer(3)
-        load_scales(nc.gpsimd, w3s, w3_scales)
+        load_first_layer(3, 4)
 
-        make_identity(nc, ident[:])
-        nc.vector.memset(own_out[0][:], 0.0)
-        nc.scalar.activation(own_out[1][:], own_out[0][:], RELU)
+        zeros = held([P, T], F32, "zeros")
+        nc.vector.memset(zeros[:], 0.0)
+        nc.scalar.activation(own_out[0][:], zeros[:], RELU)
 
         slot_words = {}
         slot_scales = {}
 
+        cuts = [0,384,768,1024]
+        pieces = {}
+
         def gather_far(e):
-            words = held([P, D], U32, "fw%d" % e)
-            scales = held([P, D], U8, "fs%d" % e)
-            cols = far_list[:, e * D // 16 : (e + 1) * D // 16]
-            nc.vector.tensor_copy(words[:], far_words[:].bitcast(U32).indirect(cols))
-            nc.vector.tensor_copy(scales[:], far_scales[:].indirect(cols))
-            slot_words["far", e] = words
-            slot_scales["far", e] = scales
+            for j in range(len(cuts) - 1):
+                if cuts[j] // D == e:
+                    first, last = cuts[j], cuts[j + 1]
+                    words = keep.tile([P, last - first], U32, name="fw%d" % j, tag="late_gw%d" % j, align_bytes=64)
+                    scales = keep.tile([P, last - first], U8, name="fs%d" % j, tag="late_gb%d" % j, align_bytes=64)
+                    cols = far_list[:, first // 16 : last // 16]
+                    nc.vector.tensor_copy(words[:], far_words[:].bitcast(U32).indirect(cols))
+                    nc.vector.tensor_copy(scales[:], far_scales[:].indirect(cols))
+                    for slot in range(first, last, P):
+                        pieces[slot] = (words[:, slot - first : slot - first + P], scales[:, slot - first : slot - first + P])
 
         pairs = [held([P, T, 2], BF16, "pairs%d" % u) for u in range(2)]
 
         def round_own(u):
             nc.scalar.copy(pairs[u][:], xo_raw[u][:].rearrange("p e c -> p c e"))
 
-        picked = held([P, 2, E * C, 2], BF16, "picked")
+        picked = [held([P, 2, PAIR, 2], BF16, "picked%d" % g) for g in range(2)]
+        grouped = [keep.tile([P, PAIR, 2, 2], BF16, name="grouped%d" % g, tag=("late_gw2", "grp1")[g], align_bytes=64) for g in range(2)]
 
-        def gather_own(u):
-            window = pairs[u][:].rearrange("p c e -> p (c e)").bitcast(U32)
-            nc.vector.tensor_copy(picked[:, u].rearrange("p c e -> p (c e)").bitcast(U32), window.indirect(own_list[:]))
-
-        grouped = [held([P, PAIR, 2, 2], BF16, "grouped%d" % g) for g in range(2)]
+        def gather_own(g):
+            cols = own_list[:, g * PAIR // 16 : (g + 1) * PAIR // 16]
+            for u in range(2):
+                window = pairs[u][:].rearrange("p c e -> p (c e)").bitcast(U32)
+                nc.vector.tensor_copy(picked[g][:, u].rearrange("p c e -> p (c e)").bitcast(U32), window.indirect(cols))
 
         def interleave_own(g):
-            nc.scalar.copy(grouped[g][:], picked[:, :, g * PAIR : (g + 1) * PAIR, :].rearrange("p u c e -> p c u e"))
+            nc.vector.tensor_copy(grouped[g][:], picked[g][:].rearrange("p u c e -> p c u e"))
 
         def quantize_own(g):
             words = held([P, PAIR], U32, "ow%d" % g)
@@ -129,24 +140,33 @@ def tile_moe_loc_glu_relu_kernel(
         def first_layer(group, half):
             e = expert_of(group, half)
             cols = slice(half * P, (half + 1) * P)
-            a1 = psum.tile([P, H], F32, name="a1", bufs=3)
+            tw, ts = pieces[group[1] * D + half * P] if group[0] == "far" else (slot_words[group][:, cols], slot_scales[group][:, cols])
+            a1 = psum.tile([P, H], F32, name="a1", bufs=2)
             a3 = psum.tile([P, H], F32, name="a3", bufs=3)
             for acc, w, ws in ((a1, w1, w1s), (a3, w3, w3s)):
                 nc.tensor.matmul_mx(
-                    acc[:], lhsT=slot_words[group][:, cols].bitcast(FP8X4), lhsT_scale=slot_scales[group][:, cols],
-                    rhs=w[e][:].bitcast(FP8X4), rhs_scale=ws[4 * e : P, :], start=True, stop=True,
+                    acc[:], lhsT=tw.bitcast(FP8X4), lhsT_scale=ts,
+                    rhs=w[:, e, :].bitcast(FP8X4), rhs_scale=ws[4 * e : P, :], start=True, stop=True,
                 )
             sums[group, half] = (a1, a3)
 
         def rectify(group, half):
-            gatev = ring.tile([P, 2, P, 2], F32, name="gatev")
+            tag = {}.get(2 * groups.index(group) + half)
+            if tag:
+                gatev = keep.tile([P, 2, P, 2], F32, name="gatev_once", tag=tag, align_bytes=64)
+            else:
+                gatev = ring.tile([P, 2, P, 2], F32, name="gatev", bufs=2)
             nc.scalar.activation(gatev[:], sums[group, half][0][:].rearrange("s (p u e) -> s u p e", u=2, e=2), RELU)
             rectified[group, half] = gatev
 
         def multiply(group, half):
             a3 = sums[group, half][1]
             gatev = rectified[group, half]
-            hid = ring.tile([P, 2, P, 2], BF16, name="hid", bufs=4, align_bytes=64)
+            tag = {9: "late_z1"}.get(2 * groups.index(group) + half)
+            if tag:
+                hid = keep.tile([P, 2, P, 2], BF16, name="hid_once", tag=tag, align_bytes=64)
+            else:
+                hid = ring.tile([P, 2, P, 2], BF16, name="hid", bufs=3, align_bytes=64)
             nc.vector.tensor_tensor(hid[:], a3[:].rearrange("s (p u e) -> s u p e", u=2, e=2), gatev[:], MULT)
             hidden[group, half] = hid
 
@@ -154,7 +174,7 @@ def tile_moe_loc_glu_relu_kernel(
         banks = {}
 
         def turn(group):
-            bank = psum.tile([P, 2, 2, P], F32, name="turn_bank")
+            bank = psum.tile([P, 2, 2, P], F32, name="turn_bank", bufs=1)
             for half in range(2):
                 for u in range(2):
                     nc.tensor.transpose(bank[:, half, u, :], hidden[group, half][:, u].rearrange("s p e -> s (p e)").bitcast(F32), ident[:])
@@ -162,7 +182,11 @@ def tile_moe_loc_glu_relu_kernel(
 
         def leave_turn(group):
             bank = banks["turn", group]
-            hT = ring.tile([P, 2, P, 2], F32, name="hT", align_bytes=64)
+            tag = {}.get(groups.index(group))
+            if tag:
+                hT = keep.tile([P, 2, P, 2], F32, name="hT_once", tag=tag, align_bytes=64)
+            else:
+                hT = ring.tile([P, 2, P, 2], F32, name="hT", align_bytes=64)
             nc.scalar.copy(hT[:], bank[:].rearrange("p a u s -> p a s u"))
             turned[group] = hT
 
@@ -178,7 +202,7 @@ def tile_moe_loc_glu_relu_kernel(
 
         def second_layer(group):
             words, scales = coded[group]
-            bank = psum.tile([P, 2, PAIR], F32, name="y_bank")
+            bank = psum.tile([P, 2, PAIR], F32, name="y_bank", bufs=2)
             spans = [slice(0, PAIR)] if group[0] == "far" else [slice(0, P), slice(P, PAIR)]
             for h in range(2):
                 rows = slice(h * P, (h + 1) * P)
@@ -193,60 +217,51 @@ def tile_moe_loc_glu_relu_kernel(
         def leave_second(group):
             bank = banks["y", group]
             y = ring.tile([P, 2, PAIR], F32, name="y", bufs=6)
-            nc.scalar.copy(y[:], bank[:])
+            if groups.index(group) in (0,):
+                nc.vector.tensor_copy(y[:], bank[:])
+            else:
+                nc.scalar.copy(y[:], bank[:])
             results[group] = y
             if group[0] == "far":
                 first = T + group[1] * D
                 nc.sync.dma_start(out[:, first : first + D].rearrange("(h p) c -> p h c", h=2), y[:])
 
-        def scatter(e, h):
-            cols = own_list[:, e * C // 16 : (e + 1) * C // 16]
-            y = results["own", e // 2][:, h, (e % 2) * C : (e % 2 + 1) * C]
-            nc.vector.tensor_tensor(own_out[h][:].indirect(cols), y, gate_sb[:, e * C : (e + 1) * C], MULT)
-            if e == E - 1:
-                nc.sync.dma_start(out[h * P : (h + 1) * P, 0:T], own_out[h][:])
+        def scatter(h, width):
+            for first in range(0, E * C, width):
+                cols = own_list[:, first // 16 : (first + width) // 16]
+                y = results["own", first // PAIR][:, h, first % PAIR : first % PAIR + width]
+                nc.vector.tensor_tensor(own_out[h][:].indirect(cols), y, gate_sb[:, first : first + width], MULT)
+            nc.sync.dma_start(out[h * P : (h + 1) * P, 0:T], own_out[h][:])
 
-        groups = [("far", 0), ("own", 0), ("far", 1), ("own", 1), ("far", 2), ("far", 3)]
+        groups = [("far", 0), ("own", 0), ("far", 1), ("far", 2), ("own", 1), ("far", 3)]
         gather_far(0)
         round_own(0)
         round_own(1)
-        gather_far(1)
-        gather_far(2)
         gather_own(0)
         gather_own(1)
-
-        fillers = {
-            (0, 1): [(interleave_own, 0), (quantize_own, 0), (interleave_own, 1)],
-            (1, 0): [(quantize_own, 1)],
-            (2, 0): [(gather_far, 3)],
-            (4, 0): [(scatter, 0, 0)],
-            (4, 1): [(scatter, 0, 1)],
-            (4, 2): [(scatter, 1, 0)],
-            (5, 2): [(scatter, 1, 1)],
-            (6, 1): [(scatter, 2, 0)],
-            (7, 0): [(scatter, 3, 0), (scatter, 2, 1), (scatter, 3, 1)],
-        }
-
-        def fill(step, slot):
-            for work, *args in fillers.get((step, slot), []):
-                work(*args)
+        for g in range(2):
+            interleave_own(g)
+            quantize_own(g)
 
         def stage(work, step, *args):
             if 0 <= step < len(groups):
                 work(groups[step], *args)
 
         for step in range(len(groups) + 2):
-            fill(step, 0)
             for half in range(2):
                 stage(first_layer, step, half)
             for half in range(2):
                 stage(rectify, step, half)
-            stage(multiply, step, 0)
-            fill(step, 1)
-            stage(multiply, step, 1)
+            for half in range(2):
+                stage(multiply, step, half)
             stage(turn, step - 1)
             stage(second_layer, step - 2)
             stage(leave_turn, step - 1)
             stage(leave_second, step - 2)
-            fill(step, 2)
+            if step + 1 < len(groups) and groups[step + 1][0] == "far":
+                gather_far(groups[step + 1][1])
             stage(quantize_hidden, step - 1)
+        own_out[1] = keep.tile([P, T], F32, name="own_out1", tag="late_z1", align_bytes=64)
+        nc.gpsimd.memset(own_out[1][:], 0.0)
+        scatter(1, 256)
+        scatter(0, 256)

from contextlib import ExitStack

import concourse.mybir as mybir
from concourse.masks import make_identity

K, T, Q, E, C, D, H, N = 512, 768, 512, 4, 128, 256, 512, 256
FLOPS = 2 * E * (C + D) * (2 * K * H + H * N)

F32 = mybir.dt.float32
BF16 = mybir.dt.bfloat16
I32 = mybir.dt.int32
U32 = mybir.dt.uint32
U16 = mybir.dt.uint16
U8 = mybir.dt.uint8
FP8X4 = mybir.dt.float8_e4m3fn_x4
MULT = mybir.AluOpType.mult
RELU = mybir.ActivationFunctionType.Relu

P = 128
PAIR = 2 * P


def tile_moe_loc_glu_relu_kernel(
    tc, x_words, x_scales, xo, w1_words, w1_scales, w3_words, w3_scales, w2_words, w2_scales, gate, offs, offs2, out
):
    nc = tc.nc
    with ExitStack() as ctx:
        keep = ctx.enter_context(tc.tile_pool(name="keep", bufs=1))
        ring = ctx.enter_context(tc.tile_pool(name="ring", bufs=3))
        psum = ctx.enter_context(tc.psum_pool(name="psum", bufs=1))

        def held(shape, dtype, name):
            return keep.tile(shape, dtype, name=name, align_bytes=64)

        def as_words(dram):
            return dram.rearrange("p n t -> p (n t)").bitcast(I32)

        own_list = keep.tile([P, E * C // 16], U16, name="own_list")
        far_list = keep.tile([P, E * D // 16], U16, name="far_list")
        far_words = held([P, Q], I32, "far_words")
        far_scales = held([P, Q], U8, "far_scales")
        xo_raw = [held([P, 2, T], F32, "xo_raw%d" % u) for u in range(2)]
        w1 = held([P, E, H], I32, "w1")
        w3 = held([P, E, H], I32, "w3")
        w2 = held([P, E, N], I32, "w2")
        w1s = held([P, H], U8, "w1s")
        w3s = held([P, H], U8, "w3s")
        w2s = held([P, N], U8, "w2s")
        gate_sb = held([P, E * C], F32, "gate_sb")
        ident = held([P, P], F32, "ident")
        own_out = {0: held([P, T], F32, "own_out0")}

        for plane in (far_scales, w1s, w3s, w2s):
            nc.vector.memset(plane[:].bitcast(I32), 0)

        def load_scales(queue, plane, dram):
            for q in range(4):
                queue.dma_start(plane[32 * q : 32 * q + 16, :].bitcast(I32), dram[:, 0, 4 * q : 4 * q + 4, :].bitcast(I32))

        def load_words(tile, dram, first, last):
            nc.sync.dma_start(tile[:, first:last, :], dram[first:last, 0].rearrange("e p n t -> p e (n t)").bitcast(I32))

        def load_first_layer(first, last):
            load_words(w1, w1_words, first, last)
            load_words(w3, w3_words, first, last)

        xo_rows = xo.rearrange("(p j) c -> p j c", j=4)
        load_scales(nc.gpsimd, w3s, w3_scales)
        make_identity(nc, ident[:])
        nc.sync.dma_start(far_list[:], offs2)
        nc.sync.dma_start(far_words[:], as_words(x_words[0]))
        for q in range(4):
            nc.sync.dma_start(far_scales[32 * q : 32 * q + 4, :].bitcast(I32), x_scales[0, 4 * q : 4 * q + 4, :].bitcast(I32))
        nc.sync.dma_start(xo_raw[0][:], xo_rows[:, 0 : 2, :])
        nc.sync.dma_start(xo_raw[1][:], xo_rows[:, 2 : 4, :])
        nc.sync.dma_start(own_list[:], offs)
        load_scales(nc.sync, w1s, w1_scales)
        load_first_layer(0, 1)
        load_first_layer(1, 2)
        load_scales(nc.sync, w2s, w2_scales)
        load_words(w2, w2_words, 0, E)
        load_first_layer(2, 3)
        nc.sync.dma_start(gate_sb[:], gate)
        load_first_layer(3, 4)

        zeros = held([P, T], F32, "zeros")
        nc.vector.memset(zeros[:], 0.0)
        nc.scalar.activation(own_out[0][:], zeros[:], RELU)

        slot_words = {}
        slot_scales = {}

        cuts = [0,384,768,1024]
        pieces = {}

        def gather_far(e):
            for j in range(len(cuts) - 1):
                if cuts[j] // D == e:
                    first, last = cuts[j], cuts[j + 1]
                    words = keep.tile([P, last - first], U32, name="fw%d" % j, tag="late_gw%d" % j, align_bytes=64)
                    scales = keep.tile([P, last - first], U8, name="fs%d" % j, tag="late_gb%d" % j, align_bytes=64)
                    cols = far_list[:, first // 16 : last // 16]
                    nc.vector.tensor_copy(words[:], far_words[:].bitcast(U32).indirect(cols))
                    nc.vector.tensor_copy(scales[:], far_scales[:].indirect(cols))
                    for slot in range(first, last, P):
                        pieces[slot] = (words[:, slot - first : slot - first + P], scales[:, slot - first : slot - first + P])

        pairs = [held([P, T, 2], BF16, "pairs%d" % u) for u in range(2)]

        def round_own(u):
            nc.scalar.copy(pairs[u][:], xo_raw[u][:].rearrange("p e c -> p c e"))

        picked = [held([P, 2, PAIR, 2], BF16, "picked%d" % g) for g in range(2)]
        grouped = [keep.tile([P, PAIR, 2, 2], BF16, name="grouped%d" % g, tag=("late_gw2", "grp1")[g], align_bytes=64) for g in range(2)]

        def gather_own(g):
            cols = own_list[:, g * PAIR // 16 : (g + 1) * PAIR // 16]
            for u in range(2):
                window = pairs[u][:].rearrange("p c e -> p (c e)").bitcast(U32)
                nc.vector.tensor_copy(picked[g][:, u].rearrange("p c e -> p (c e)").bitcast(U32), window.indirect(cols))

        def interleave_own(g):
            nc.vector.tensor_copy(grouped[g][:], picked[g][:].rearrange("p u c e -> p c u e"))

        def quantize_own(g):
            words = held([P, PAIR], U32, "ow%d" % g)
            scales = held([P, PAIR], U8, "os%d" % g)
            nc.vector.quantize_mx(words[:].bitcast(FP8X4), scales[:], grouped[g][:].rearrange("p c u e -> p (c u e)"))
            slot_words["own", g] = words
            slot_scales["own", g] = scales

        def expert_of(group, half):
            kind, g = group
            return g if kind == "far" else 2 * g + half

        hidden = {}
        sums = {}
        rectified = {}

        def first_layer(group, half):
            e = expert_of(group, half)
            cols = slice(half * P, (half + 1) * P)
            tw, ts = pieces[group[1] * D + half * P] if group[0] == "far" else (slot_words[group][:, cols], slot_scales[group][:, cols])
            a1 = psum.tile([P, H], F32, name="a1", bufs=2)
            a3 = psum.tile([P, H], F32, name="a3", bufs=3)
            for acc, w, ws in ((a1, w1, w1s), (a3, w3, w3s)):
                nc.tensor.matmul_mx(
                    acc[:], lhsT=tw.bitcast(FP8X4), lhsT_scale=ts,
                    rhs=w[:, e, :].bitcast(FP8X4), rhs_scale=ws[4 * e : P, :], start=True, stop=True,
                )
            sums[group, half] = (a1, a3)

        def rectify(group, half):
            tag = {}.get(2 * groups.index(group) + half)
            if tag:
                gatev = keep.tile([P, 2, P, 2], F32, name="gatev_once", tag=tag, align_bytes=64)
            else:
                gatev = ring.tile([P, 2, P, 2], F32, name="gatev", bufs=2)
            nc.scalar.activation(gatev[:], sums[group, half][0][:].rearrange("s (p u e) -> s u p e", u=2, e=2), RELU)
            rectified[group, half] = gatev

        def multiply(group, half):
            a3 = sums[group, half][1]
            gatev = rectified[group, half]
            tag = {9: "late_z1"}.get(2 * groups.index(group) + half)
            if tag:
                hid = keep.tile([P, 2, P, 2], BF16, name="hid_once", tag=tag, align_bytes=64)
            else:
                hid = ring.tile([P, 2, P, 2], BF16, name="hid", bufs=3, align_bytes=64)
            nc.vector.tensor_tensor(hid[:], a3[:].rearrange("s (p u e) -> s u p e", u=2, e=2), gatev[:], MULT)
            hidden[group, half] = hid

        turned = {}
        banks = {}

        def turn(group):
            bank = psum.tile([P, 2, 2, P], F32, name="turn_bank", bufs=1)
            for half in range(2):
                for u in range(2):
                    nc.tensor.transpose(bank[:, half, u, :], hidden[group, half][:, u].rearrange("s p e -> s (p e)").bitcast(F32), ident[:])
            banks["turn", group] = bank

        def leave_turn(group):
            bank = banks["turn", group]
            tag = {}.get(groups.index(group))
            if tag:
                hT = keep.tile([P, 2, P, 2], F32, name="hT_once", tag=tag, align_bytes=64)
            else:
                hT = ring.tile([P, 2, P, 2], F32, name="hT", align_bytes=64)
            nc.scalar.copy(hT[:], bank[:].rearrange("p a u s -> p a s u"))
            turned[group] = hT

        coded = {}

        def quantize_hidden(group):
            words = ring.tile([P, PAIR], U32, name="hw", align_bytes=64)
            scales = ring.tile([P, PAIR], U8, name="hs", align_bytes=64)
            nc.vector.quantize_mx(words[:].bitcast(FP8X4), scales[:], turned[group][:].rearrange("p a s u -> p (a s u)").bitcast(BF16))
            coded[group] = (words, scales)

        results = {}

        def second_layer(group):
            words, scales = coded[group]
            bank = psum.tile([P, 2, PAIR], F32, name="y_bank", bufs=2)
            spans = [slice(0, PAIR)] if group[0] == "far" else [slice(0, P), slice(P, PAIR)]
            for h in range(2):
                rows = slice(h * P, (h + 1) * P)
                for half, span in enumerate(spans):
                    e = expert_of(group, half)
                    nc.tensor.matmul_mx(
                        bank[:, h, span], lhsT=w2[:, e, rows].bitcast(FP8X4), lhsT_scale=w2s[4 * e : P, rows],
                        rhs=words[:, span].bitcast(FP8X4), rhs_scale=scales[:, span], start=True, stop=True,
                    )
            banks["y", group] = bank

        def leave_second(group):
            bank = banks["y", group]
            y = ring.tile([P, 2, PAIR], F32, name="y", bufs=6)
            if groups.index(group) in (0,):
                nc.vector.tensor_copy(y[:], bank[:])
            else:
                nc.scalar.copy(y[:], bank[:])
            results[group] = y
            if group[0] == "far":
                first = T + group[1] * D
                nc.sync.dma_start(out[:, first : first + D].rearrange("(h p) c -> p h c", h=2), y[:])

        def scatter(h, width):
            for first in range(0, E * C, width):
                cols = own_list[:, first // 16 : (first + width) // 16]
                y = results["own", first // PAIR][:, h, first % PAIR : first % PAIR + width]
                nc.vector.tensor_tensor(own_out[h][:].indirect(cols), y, gate_sb[:, first : first + width], MULT)
            nc.sync.dma_start(out[h * P : (h + 1) * P, 0:T], own_out[h][:])

        groups = [("far", 0), ("own", 0), ("far", 1), ("far", 2), ("own", 1), ("far", 3)]
        gather_far(0)
        round_own(0)
        round_own(1)
        gather_own(0)
        gather_own(1)
        for g in range(2):
            interleave_own(g)
            quantize_own(g)

        def stage(work, step, *args):
            if 0 <= step < len(groups):
                work(groups[step], *args)

        for step in range(len(groups) + 2):
            for half in range(2):
                stage(first_layer, step, half)
            for half in range(2):
                stage(rectify, step, half)
            for half in range(2):
                stage(multiply, step, half)
            stage(turn, step - 1)
            stage(second_layer, step - 2)
            stage(leave_turn, step - 1)
            stage(leave_second, step - 2)
            if step + 1 < len(groups) and groups[step + 1][0] == "far":
                gather_far(groups[step + 1][1])
            stage(quantize_hidden, step - 1)
        own_out[1] = keep.tile([P, T], F32, name="own_out1", tag="late_z1", align_bytes=64)
        nc.gpsimd.memset(own_out[1][:], 0.0)
        scatter(1, 256)
        scatter(0, 256)
